import numpy as np
import ml_dtypes


def mxq(x, axis, fmt="e4m3"):
    dtype, down = {"e4m3": (ml_dtypes.float8_e4m3fn, 7), "e5m2": (ml_dtypes.float8_e5m2, 14)}[fmt]
    v = np.moveaxis(np.asarray(x, np.float32).astype(ml_dtypes.bfloat16).astype(np.float64), axis, -1)
    blocks = v.reshape(v.shape[:-1] + (-1, 32))
    amax = np.abs(blocks).max(-1, keepdims=True)
    byte = np.maximum(np.where(amax > 0, np.frexp(amax)[1] - 1 + 127, 0) - down, 1)
    scale = np.exp2(byte - 127.0)
    codes = (blocks / scale).astype(np.float32).astype(dtype).astype(np.float64)
    return np.moveaxis((codes * scale).reshape(v.shape), -1, axis)


WIDE = False


def mx_kscale(k):
    if not WIDE:
        return np.ones(k)
    levels = np.array([10, -10, 5, -5, 0])
    if k % 512:
        return np.exp2(np.random.permutation(np.resize(levels, k // 32))).repeat(32)
    a = np.empty((k // 512, 16))
    for p in range(k // 512):
        a[p, :8] = np.random.permutation(np.resize(levels, 8))
        for g in range(8):
            far = levels[np.abs(levels - a[p, g]) >= 10]
            a[p, g + 8] = far[np.random.randint(len(far))]
    return np.exp2(a.ravel()).repeat(32)


def f64(x):
    return np.asarray(x).astype(np.float64)


def striped(idx):
    return np.tile(idx.reshape(-1, 16).T, (8, 1)).astype(np.uint16)


def unstriped(offs):
    return offs[:16].T.reshape(-1).astype(np.int64)


E2M1 = np.array([0.0, 0.5, 1.0, 1.5, 2.0, 3.0, 4.0, 6.0, -0.0, -0.5, -1.0, -1.5, -2.0, -3.0, -4.0, -6.0])


def pack_fp4(w):
    k, n = w.shape
    w = f64(np.asarray(w, np.float32).astype(ml_dtypes.bfloat16)).reshape(k // 32, 32, n)
    amax = np.abs(w).max(1)
    mant, ex = np.frexp(amax / 6.0)
    byte = np.clip(np.where(amax > 0, np.where(mant > 0.5, ex, ex - 1) + 127, 1), 1, 254)
    scaled = (w * np.exp2(127.0 - byte)[:, None, :]).reshape(k, n).astype(np.float32)
    c = np.ascontiguousarray(scaled.reshape(k // 512, 128, 4, n).transpose(0, 1, 3, 2)).astype(ml_dtypes.float4_e2m1fn).view(np.uint8) & 0xF
    words = (c[..., 0::2] | (c[..., 1::2] << 4)).reshape(k // 512, 128, 2 * n)
    return np.ascontiguousarray(words), np.ascontiguousarray(byte.astype(np.uint8).reshape(k // 512, 16, n))


def unpack_fp4(words, scales):
    g, _, n = scales.shape
    words = np.ascontiguousarray(words).reshape(g, 128, n, 2)
    nib = np.empty((g, 128, n, 4), np.uint8)
    nib[..., 0::2] = words & 0xF
    nib[..., 1::2] = words >> 4
    vals = E2M1[nib] * np.repeat(np.exp2(scales.astype(np.float64) - 127.0), 8, axis=1)[..., None]
    return vals.transpose(0, 1, 3, 2).reshape(g * 512, n)


def relu(v):
    return np.maximum(v, 0.0)


K, T, S, V, H, N = 1024, 2048, 1024, 512, 512, 256


def setup_inputs():
    n = np.random.standard_normal
    s = mx_kscale(K)[:, None]
    u = mx_kscale(H)
    packed_w2 = pack_fp4(n((H, N)) / np.sqrt(2 * H) / u[:, None])
    packed_w3 = pack_fp4(n((H, N)) / np.sqrt(2 * H) / u[:, None])
    return {
        "xT": (n((K, T)) * s).astype(np.float32),
        "w1": (n((K, H)) / np.sqrt(K) / s * u).astype(np.float32),
        "w2_words": packed_w2[0],
        "w2_scales": packed_w2[1],
        "w3_words": packed_w3[0],
        "w3_scales": packed_w3[1],
        "offs": striped(np.random.permutation(T)[:S]),
        "cen": striped(np.random.permutation(S)[:V]),
        "pos1": striped(np.random.permutation(S)[:V]),
        "pos2": striped(np.random.permutation(S)[:V]),
    }


def reference(xT, w1, w2_words, w2_scales, w3_words, w3_scales, offs, cen, pos1, pos2):
    xq = mxq(f64(xT)[:, unstriped(offs)], 0, "e4m3")
    h = relu(mxq(f64(w1), 0, "e4m3").T @ xq)
    hc = h[:, unstriped(cen)]
    z = np.maximum(h[:, unstriped(pos1)], h[:, unstriped(pos2)])
    return unpack_fp4(w2_words, w2_scales).T @ mxq(hc, 0, "e4m3") + unpack_fp4(w3_words, w3_scales).T @ mxq(z, 0, "e4m3")

@@ -1,0 +1,229 @@
+from contextlib import ExitStack
+
+import concourse.mybir as mybir
+
+K, T, S, V, H, N = 1024, 2048, 1024, 512, 512, 256
+FLOPS = 2 * K * H * S + 2 * 2 * H * N * V
+
+F32 = mybir.dt.float32
+BF16 = mybir.dt.bfloat16
+U32 = mybir.dt.uint32
+I32 = mybir.dt.int32
+U16 = mybir.dt.uint16
+U8 = mybir.dt.uint8
+FP8X4 = mybir.dt.float8_e4m3fn_x4
+FP4X4 = mybir.dt.float4_e2m1fn_x4
+COPY = mybir.ActivationFunctionType.Copy
+RELU = mybir.ActivationFunctionType.Relu
+MAX = mybir.AluOpType.max
+
+P = 128
+PACK = 4
+K_PASS = P * PACK
+PASSES = K // K_PASS
+BANK = 512
+LIST_ROWS = 16
+X_CHUNKS = ((1024, 512, 512), (1024, 512, 256, 256))
+W_CHUNK = 256
+V_GROUP = 128
+
+
+def weave_views(woven, planes):
+    return (
+        woven.rearrange("p (c i) j -> p c j i", i=4),
+        planes.rearrange("p j (c i) -> p c j i", i=4),
+    )
+
+
+def quantize(nc, words, scale_bytes, woven):
+    nc.vector.quantize_mx(out=words.bitcast(FP8X4), scales=scale_bytes, in_=woven.rearrange("p c j -> p (c j)"))
+
+
+def tile_picked_sagecat_max_e_kernel(
+    tc, xT, w1, w2_words, w2_scales, w3_words, w3_scales, offs, cen, pos1, pos2, out
+):
+    nc = tc.nc
+    with ExitStack() as ctx:
+        sb = ctx.enter_context(tc.tile_pool(name="sb", bufs=1))
+        psum = ctx.enter_context(tc.psum_pool(name="psum", bufs=1))
+
+        def list_tile(name, src):
+            t = sb.tile(list(src.shape), U16, name=name)
+            nc.sync.dma_start(t[:], src)
+            return t
+
+        x_raw = []
+        offs_sb = None
+        for z in range(PASSES):
+            rows = xT[z * K_PASS : (z + 1) * K_PASS, :].rearrange("(p j) c -> p j c", j=PACK)
+            c0 = 0
+            for width in X_CHUNKS[z]:
+                raw = sb.tile([P, PACK, width], F32, name=f"x_raw_{z}_{c0}")
+                nc.sync.dma_start(raw[:], rows[:, :, c0 : c0 + width])
+                x_raw.append((z, c0, width, raw))
+                c0 = c0 + width
+            if z == 0:
+                offs_sb = list_tile("offs_sb", offs)
+        w_raw = []
+        for z in range(PASSES):
+            rows = w1[z * K_PASS : (z + 1) * K_PASS, :].rearrange("(p j) c -> p j c", j=PACK)
+            for c0 in range(0, H, W_CHUNK):
+                raw = sb.tile([P, PACK, W_CHUNK], F32, name=f"w_raw_{z}_{c0}")
+                nc.sync.dma_start(raw[:], rows[:, :, c0 : c0 + W_CHUNK])
+                w_raw.append((z, c0, raw))
+        pos1_sb = list_tile("pos1_sb", pos1)
+        pos2_sb = list_tile("pos2_sb", pos2)
+        cen_sb = list_tile("cen_sb", cen)
+
+        x_bytes = sb.tile([P, T], U8, name="x_bytes", align_bytes=64)
+        nc.gpsimd.memset(x_bytes[:], 0)
+        fp4_words, fp4_bytes = [], []
+        for name, words, scales in (("w3", w3_words, w3_scales), ("w2", w2_words, w2_scales)):
+            wt = sb.tile([P, 2 * N], U8, name=name + "_words", align_bytes=64)
+            nc.sync.dma_start(wt[:].bitcast(I32), words[0].bitcast(I32))
+            st = sb.tile([P, N], U8, name=name + "_bytes", align_bytes=64)
+            nc.gpsimd.memset(st[:], 0)
+            for q in range(4):
+                nc.sync.dma_start(
+                    st[32 * q : 32 * q + 4, :].bitcast(I32), scales[0, 4 * q : 4 * q + 4, :].bitcast(I32)
+                )
+            fp4_words.append(wt)
+            fp4_bytes.append(st)
+
+        x_words = [sb.tile([P, T], U32, name=f"x_words_{z}", align_bytes=64) for z in range(PASSES)]
+        g_words = [sb.tile([P, S], U32, name="g_words_0", align_bytes=64)]
+        g_bytes = sb.tile([P, S], U8, name="g_bytes", align_bytes=64)
+        for z, c0, width, raw in x_raw:
+            half = width // 2
+            by_scalar = sb.tile([P, half, PACK], BF16, name=f"xs_{z}_{c0}", align_bytes=64)
+            by_vector = sb.tile([P, half, PACK], BF16, name=f"xv_{z}_{c0}", align_bytes=64)
+            dst, src = weave_views(by_scalar[:], raw[:, :, 0:half])
+            nc.scalar.activation(dst, src, COPY)
+            dst, src = weave_views(by_vector[:], raw[:, :, half:width])
+            nc.vector.tensor_copy(dst, src)
+            for woven, lo in ((by_vector, c0 + half), (by_scalar, c0)):
+                quantize(nc, x_words[z][:, lo : lo + half], x_bytes[4 * z : P, lo : lo + half], woven[:])
+            if z == 0 and c0 + width == T:
+                nc.vector.tensor_copy(g_words[0][:], x_words[0][:].indirect(offs_sb[:]))
+
+        w_woven = [sb.tile([P, PACK, P, PACK], BF16, name=f"w_woven_{z}", tag=f"w_woven_{z}", align_bytes=64) for z in range(PASSES)]
+        w_words = [sb.tile([P, H], U32, name=f"w_words_{z}", align_bytes=64) for z in range(PASSES)]
+        w_bytes = [sb.tile([P, H], U8, name=f"w_bytes_{z}", align_bytes=64) for z in range(PASSES)]
+        for z, c0, raw in w_raw:
+            m0, m1 = c0 // PACK, (c0 + W_CHUNK) // PACK
+            nc.scalar.activation(
+                w_woven[z][:, :, m0:m1, :].rearrange("p t m j -> p m j t"),
+                raw[:].rearrange("p j (m t) -> p m j t", t=PACK),
+                COPY,
+            )
+
+        nc.vector.tensor_copy(g_bytes[:], x_bytes[:].indirect(offs_sb[:]))
+        quantize(nc, w_words[0][:], w_bytes[0][:], w_woven[0][:].rearrange("p t m j -> p (t m) j"))
+        g_words.append(sb.tile([P, S], U32, name="g_words_1", tag="w_woven_0", align_bytes=64))
+        cols = BANK // LIST_ROWS
+        for half in range(S // BANK):
+            nc.vector.tensor_copy(
+                g_words[1][:, half * BANK : (half + 1) * BANK],
+                x_words[1][:].indirect(offs_sb[:, half * cols : (half + 1) * cols]),
+            )
+        for t in range(PACK):
+            quantize(nc, w_words[1][:, t * P : (t + 1) * P], w_bytes[1][:, t * P : (t + 1) * P], w_woven[1][:, t])
+
+        acc = [
+            [psum.tile([P, BANK], F32, name=f"acc_{t}_{half}", tag=f"bank_{t}_{half}") for half in range(2)]
+            for t in range(PACK)
+        ]
+        h = [sb.tile([P, S], F32, name=f"h_{t}") for t in range(PACK)]
+
+        def first_pass(z, t, half):
+            wc = slice(t * P, (t + 1) * P)
+            xc = slice(half * BANK, (half + 1) * BANK)
+            nc.tensor.matmul_mx(
+                out=acc[t][half][:],
+                lhsT=w_words[z][:, wc].bitcast(FP8X4),
+                lhsT_scale=w_bytes[z][:, wc],
+                rhs=g_words[z][:, xc].bitcast(FP8X4),
+                rhs_scale=g_bytes[4 * z : P, xc],
+                start=(z == 0),
+                stop=(z == PASSES - 1),
+            )
+
+        for t in range(PACK):
+            for half in range(2):
+                first_pass(0, t, half)
+        for t in range(PACK):
+            for half in range(2):
+                first_pass(1, t, half)
+                dst = h[t][:, half * BANK : (half + 1) * BANK]
+                if t == 0 and half == 1:
+                    nc.vector.tensor_scalar_max(dst, acc[t][half][:], 0.0)
+                else:
+                    nc.scalar.activation(dst, acc[t][half][:], RELU)
+
+        largest = sb.tile([P, PACK, V], BF16, name="largest", tag="largest", align_bytes=64)
+        for t in range(PACK):
+            near1 = sb.tile([P, V], BF16, name=f"near1_{t}", tag=f"near1_{t}", align_bytes=64)
+            near2 = sb.tile([P, V], BF16, name=f"near2_{t}", tag=f"near2_{t}", align_bytes=64)
+            nc.vector.tensor_copy(near1[:], h[t][:].indirect(pos1_sb[:]))
+            nc.vector.tensor_copy(near2[:], h[t][:].indirect(pos2_sb[:]))
+            nc.vector.tensor_tensor(largest[:, t, :], near1[:], near2[:], MAX)
+        z_woven = sb.tile([P, V, PACK], BF16, name="z_woven", tag="z_woven", align_bytes=64)
+        dst, src = weave_views(z_woven[:], largest[:])
+        nc.scalar.copy(dst, src)
+
+        groups = V // V_GROUP
+        plane_tags = ("centre_0", "near1_3", "near2_3", "z_woven")
+        woven_tags = ("largest", "c_woven_1", "c_woven_2", "c_woven_3")
+        z_words = sb.tile([P, V], U32, name="z_words", align_bytes=64)
+        z_bytes = sb.tile([P, V], U8, name="z_bytes", align_bytes=64)
+        res = {}
+
+        def second_pass(which, words, scale_bytes, g, mt):
+            nc.tensor.matmul_mx(
+                out=res[g, mt][:],
+                lhsT=fp4_words[which][:, 2 * P * mt : 2 * P * (mt + 1)].bitcast(FP4X4),
+                lhsT_scale=fp4_bytes[which][:, P * mt : P * (mt + 1)],
+                rhs=words.bitcast(FP8X4),
+                rhs_scale=scale_bytes,
+                start=(which == 0),
+                stop=(which == 1),
+            )
+
+        def finish(g, woven):
+            words = sb.tile([P, V_GROUP], U32, name=f"c_words_{g}", align_bytes=64)
+            scale_bytes = sb.tile([P, V_GROUP], U8, name=f"c_bytes_{g}", align_bytes=64)
+            quantize(nc, words[:], scale_bytes[:], woven[:])
+            staged = sb.tile([P, N // P, V_GROUP], F32, name=f"staged_{g}")
+            for mt in range(N // P):
+                second_pass(1, words[:], scale_bytes[:], g, mt)
+                if g == groups - 1 and mt == 1:
+                    nc.vector.tensor_copy(staged[:, mt, :], res[g, mt][:])
+                else:
+                    nc.scalar.copy(staged[:, mt, :], res[g, mt][:])
+            nc.sync.dma_start(
+                out[:, g * V_GROUP : (g + 1) * V_GROUP].rearrange("(a p) v -> p a v", p=P), staged[:]
+            )
+
+        cols = V_GROUP // LIST_ROWS
+        wovens = []
+        for g in range(groups):
+            last = g == groups - 1
+            if last:
+                quantize(nc, z_words[:], z_bytes[:], z_woven[:])
+                for zg in range(groups):
+                    vc = slice(zg * V_GROUP, (zg + 1) * V_GROUP)
+                    for mt in range(N // P):
+                        res[zg, mt] = psum.tile([P, V_GROUP], F32, name=f"res_{zg}_{mt}", tag=f"bank_{zg}_{mt}")
+                        second_pass(0, z_words[:, vc], z_bytes[:, vc], zg, mt)
+            planes = sb.tile([P, PACK, V_GROUP], BF16, name=f"centre_{g}", tag=plane_tags[g], align_bytes=64)
+            for t in range(PACK):
+                nc.vector.tensor_copy(planes[:, t, :], h[t][:].indirect(cen_sb[:, g * cols : (g + 1) * cols]))
+            woven = sb.tile([P, V_GROUP, PACK], BF16, name=f"c_woven_{g}", tag=woven_tags[g], align_bytes=64)
+            dst, src = weave_views(woven[:], planes[:])
+            if last:
+                nc.vector.tensor_copy(dst, src)
+            else:
+                nc.scalar.copy(dst, src)
+            wovens.append(woven)
+        for g in range(groups):
+            finish(g, wovens[g])

@@ -23,9 +23,11 @@ K_PASS = P * PACK
 PASSES = K // K_PASS
 BANK = 512
 LIST_ROWS = 16
-X_CHUNKS = ((1024, 512, 512), (1024, 512, 256, 256))
-W_CHUNK = 256
+X_CHUNKS = ((1024, 512, 512), (512, 512, 512, 256, 128, 128))
+W_CHUNKS = ((128, 128, 256), (256, 256))
+MIN_SHARE = 128
 V_GROUP = 128
+V_SLICES = ((0, 128), (128, 256), (384, 128))
 
 
 def weave_views(woven, planes):
@@ -67,10 +69,12 @@ def tile_picked_sagecat_max_e_kernel(
         w_raw = []
         for z in range(PASSES):
             rows = w1[z * K_PASS : (z + 1) * K_PASS, :].rearrange("(p j) c -> p j c", j=PACK)
-            for c0 in range(0, H, W_CHUNK):
-                raw = sb.tile([P, PACK, W_CHUNK], F32, name=f"w_raw_{z}_{c0}")
-                nc.sync.dma_start(raw[:], rows[:, :, c0 : c0 + W_CHUNK])
-                w_raw.append((z, c0, raw))
+            c0 = 0
+            for width in W_CHUNKS[z]:
+                raw = sb.tile([P, PACK, width], F32, name=f"w_raw_{z}_{c0}", tag=f"w_raw_{z}_{c0}", align_bytes=64)
+                nc.sync.dma_start(raw[:], rows[:, :, c0 : c0 + width])
+                w_raw.append((z, c0, width, raw))
+                c0 = c0 + width
         pos1_sb = list_tile("pos1_sb", pos1)
         pos2_sb = list_tile("pos2_sb", pos2)
         cen_sb = list_tile("cen_sb", cen)
@@ -94,23 +98,37 @@ def tile_picked_sagecat_max_e_kernel(
         g_words = [sb.tile([P, S], U32, name="g_words_0", align_bytes=64)]
         g_bytes = sb.tile([P, S], U8, name="g_bytes", align_bytes=64)
         for z, c0, width, raw in x_raw:
-            half = width // 2
-            by_scalar = sb.tile([P, half, PACK], BF16, name=f"xs_{z}_{c0}", align_bytes=64)
-            by_vector = sb.tile([P, half, PACK], BF16, name=f"xv_{z}_{c0}", align_bytes=64)
-            dst, src = weave_views(by_scalar[:], raw[:, :, 0:half])
-            nc.scalar.activation(dst, src, COPY)
-            dst, src = weave_views(by_vector[:], raw[:, :, half:width])
-            nc.vector.tensor_copy(dst, src)
-            for woven, lo in ((by_vector, c0 + half), (by_scalar, c0)):
-                quantize(nc, x_words[z][:, lo : lo + half], x_bytes[4 * z : P, lo : lo + half], woven[:])
+            if width > MIN_SHARE:
+                shares = ((width // 2, width // 2, True), (0, width // 2, False))
+            else:
+                shares = ((0, width, c0 + width == T),)
+            rounded = []
+            for lo, n, on_vector in shares:
+                woven = sb.tile([P, n, PACK], BF16, name=f"x_woven_{z}_{c0 + lo}", align_bytes=64)
+                dst, src = weave_views(woven[:], raw[:, :, lo : lo + n])
+                if on_vector:
+                    nc.vector.tensor_copy(dst, src)
+                else:
+                    nc.scalar.activation(dst, src, COPY)
+                rounded.append((c0 + lo, n, woven))
+            for lo, n, woven in rounded:
+                quantize(nc, x_words[z][:, lo : lo + n], x_bytes[4 * z : P, lo : lo + n], woven[:])
             if z == 0 and c0 + width == T:
                 nc.vector.tensor_copy(g_words[0][:], x_words[0][:].indirect(offs_sb[:]))
 
         w_woven = [sb.tile([P, PACK, P, PACK], BF16, name=f"w_woven_{z}", tag=f"w_woven_{z}", align_bytes=64) for z in range(PASSES)]
+
         w_words = [sb.tile([P, H], U32, name=f"w_words_{z}", align_bytes=64) for z in range(PASSES)]
-        w_bytes = [sb.tile([P, H], U8, name=f"w_bytes_{z}", align_bytes=64) for z in range(PASSES)]
-        for z, c0, raw in w_raw:
-            m0, m1 = c0 // PACK, (c0 + W_CHUNK) // PACK
+        w_bytes = {}
+
+        def quantize_w1(z, t0, t1, scale_bytes):
+            wc = slice(t0 * P, t1 * P)
+            quantize(nc, w_words[z][:, wc], scale_bytes[:, wc], w_woven[z][:, t0:t1].rearrange("p t m j -> p (t m) j"))
+            for t in range(t0, t1):
+                w_bytes[z, t] = scale_bytes[:, t * P : (t + 1) * P]
+
+        for z, c0, width, raw in w_raw:
+            m0, m1 = c0 // PACK, (c0 + width) // PACK
             nc.scalar.activation(
                 w_woven[z][:, :, m0:m1, :].rearrange("p t m j -> p m j t"),
                 raw[:].rearrange("p j (m t) -> p m j t", t=PACK),
@@ -118,112 +136,142 @@ def tile_picked_sagecat_max_e_kernel(
             )
 
         nc.vector.tensor_copy(g_bytes[:], x_bytes[:].indirect(offs_sb[:]))
-        quantize(nc, w_words[0][:], w_bytes[0][:], w_woven[0][:].rearrange("p t m j -> p (t m) j"))
-        g_words.append(sb.tile([P, S], U32, name="g_words_1", tag="w_woven_0", align_bytes=64))
         cols = BANK // LIST_ROWS
-        for half in range(S // BANK):
-            nc.vector.tensor_copy(
-                g_words[1][:, half * BANK : (half + 1) * BANK],
-                x_words[1][:].indirect(offs_sb[:, half * cols : (half + 1) * cols]),
-            )
-        for t in range(PACK):
-            quantize(nc, w_words[1][:, t * P : (t + 1) * P], w_bytes[1][:, t * P : (t + 1) * P], w_woven[1][:, t])
+        late_words = []
+        for half, tag in enumerate(("late_words_0", f"w_raw_0_{H - W_CHUNKS[0][-1]}")):
+            if half == 1:
+                quantize_w1(0, 0, 1, sb.tile([P, P], U8, name="w_bytes_first", align_bytes=64))
+            picked = sb.tile([P, BANK], U32, name=f"late_words_{half}", tag=tag, align_bytes=64)
+            nc.vector.tensor_copy(picked[:], x_words[1][:].indirect(offs_sb[:, half * cols : (half + 1) * cols]))
+            late_words.append(picked)
+        w_bytes_late = sb.tile([P, H], U8, name="w_bytes_late", align_bytes=64)
+        w_bytes_rest = sb.tile([P, H], U8, name="w_bytes_rest", tag=f"w_raw_1_{H - W_CHUNKS[1][-1]}", align_bytes=64)
+        quantize_w1(1, 0, 1, w_bytes_late)
+        for t0, t1 in ((1, 2), (2, PACK)):
+            quantize_w1(1, t0, t1, w_bytes_late)
+            quantize_w1(0, t0, t1, w_bytes_rest)
 
+        warm = psum.tile([P, BANK], F32, name="warm", tag="bank_3_1")
+        for rep in range(3):
+            nc.tensor.matmul_mx(
+                out=warm[:],
+                lhsT=g_words[0][:, 0:P].bitcast(FP8X4),
+                lhsT_scale=g_bytes[:, 0:P],
+                rhs=g_words[0][:, 0:BANK].bitcast(FP8X4),
+                rhs_scale=g_bytes[:, 0:BANK],
+                start=True,
+                stop=True,
+            )
         acc = [
             [psum.tile([P, BANK], F32, name=f"acc_{t}_{half}", tag=f"bank_{t}_{half}") for half in range(2)]
             for t in range(PACK)
         ]
         h = [sb.tile([P, S], F32, name=f"h_{t}") for t in range(PACK)]
 
-        def first_pass(z, t, half):
+        def first_pass(z, t, half, opens):
             wc = slice(t * P, (t + 1) * P)
             xc = slice(half * BANK, (half + 1) * BANK)
             nc.tensor.matmul_mx(
                 out=acc[t][half][:],
                 lhsT=w_words[z][:, wc].bitcast(FP8X4),
-                lhsT_scale=w_bytes[z][:, wc],
-                rhs=g_words[z][:, xc].bitcast(FP8X4),
+                lhsT_scale=w_bytes[z, t],
+                rhs=(g_words[0][:, xc] if z == 0 else late_words[half][:]).bitcast(FP8X4),
                 rhs_scale=g_bytes[4 * z : P, xc],
-                start=(z == 0),
-                stop=(z == PASSES - 1),
+                start=opens,
+                stop=not opens,
             )
 
+        for half in range(2):
+            first_pass(0, 0, half, True)
         for t in range(PACK):
             for half in range(2):
-                first_pass(0, t, half)
-        for t in range(PACK):
-            for half in range(2):
-                first_pass(1, t, half)
-                dst = h[t][:, half * BANK : (half + 1) * BANK]
-                if t == 0 and half == 1:
-                    nc.vector.tensor_scalar_max(dst, acc[t][half][:], 0.0)
+                if t == 0:
+                    first_pass(1, t, half, False)
                 else:
-                    nc.scalar.activation(dst, acc[t][half][:], RELU)
+                    first_pass(1, t, half, True)
+                    first_pass(0, t, half, False)
+                dst = h[t][:, half * BANK : (half + 1) * BANK]
+                nc.scalar.activation(dst, acc[t][half][:], RELU)
 
-        largest = sb.tile([P, PACK, V], BF16, name="largest", tag="largest", align_bytes=64)
-        for t in range(PACK):
-            near1 = sb.tile([P, V], BF16, name=f"near1_{t}", tag=f"near1_{t}", align_bytes=64)
-            near2 = sb.tile([P, V], BF16, name=f"near2_{t}", tag=f"near2_{t}", align_bytes=64)
-            nc.vector.tensor_copy(near1[:], h[t][:].indirect(pos1_sb[:]))
-            nc.vector.tensor_copy(near2[:], h[t][:].indirect(pos2_sb[:]))
-            nc.vector.tensor_tensor(largest[:, t, :], near1[:], near2[:], MAX)
-        z_woven = sb.tile([P, V, PACK], BF16, name="z_woven", tag="z_woven", align_bytes=64)
-        dst, src = weave_views(z_woven[:], largest[:])
-        nc.scalar.copy(dst, src)
+        def gather_centres(planes, t, v0, width):
+            nc.vector.tensor_copy(
+                planes[:, t, :], h[t][:].indirect(cen_sb[:, v0 // LIST_ROWS : (v0 + width) // LIST_ROWS])
+            )
 
-        groups = V // V_GROUP
-        plane_tags = ("centre_0", "near1_3", "near2_3", "z_woven")
-        woven_tags = ("largest", "c_woven_1", "c_woven_2", "c_woven_3")
-        z_words = sb.tile([P, V], U32, name="z_words", align_bytes=64)
-        z_bytes = sb.tile([P, V], U8, name="z_bytes", align_bytes=64)
+        def weave(engine_copy, name, planes, width):
+            woven = sb.tile([P, width, PACK], BF16, name=name, tag=name, align_bytes=64)
+            dst, src = weave_views(woven[:], planes[:])
+            engine_copy(dst, src)
+            return woven
+
+        def quantized(name, woven, width):
+            words = sb.tile([P, width], U32, name=name + "_words", align_bytes=64)
+            scale_bytes = sb.tile([P, width], U8, name=name + "_bytes", align_bytes=64)
+            quantize(nc, words[:], scale_bytes[:], woven[:])
+            return words, scale_bytes
+
         res = {}
 
-        def second_pass(which, words, scale_bytes, g, mt):
-            nc.tensor.matmul_mx(
-                out=res[g, mt][:],
-                lhsT=fp4_words[which][:, 2 * P * mt : 2 * P * (mt + 1)].bitcast(FP4X4),
-                lhsT_scale=fp4_bytes[which][:, P * mt : P * (mt + 1)],
-                rhs=words.bitcast(FP8X4),
-                rhs_scale=scale_bytes,
-                start=(which == 0),
-                stop=(which == 1),
-            )
+        def second_pass(which, codes, width, v0):
+            words, scale_bytes = codes
+            for c0 in range(0, width, V_GROUP):
+                g = (v0 + c0) // V_GROUP
+                for mt in range(N // P):
+                    if which == 0:
+                        res[g, mt] = psum.tile([P, V_GROUP], F32, name=f"res_{g}_{mt}", tag=f"bank_{g}_{mt}")
+                    nc.tensor.matmul_mx(
+                        out=res[g, mt][:],
+                        lhsT=fp4_words[which][:, 2 * P * mt : 2 * P * (mt + 1)].bitcast(FP4X4),
+                        lhsT_scale=fp4_bytes[which][:, P * mt : P * (mt + 1)],
+                        rhs=words[:, c0 : c0 + V_GROUP].bitcast(FP8X4),
+                        rhs_scale=scale_bytes[:, c0 : c0 + V_GROUP],
+                        start=(which == 0),
+                        stop=(which == 1),
+                    )
 
-        def finish(g, woven):
-            words = sb.tile([P, V_GROUP], U32, name=f"c_words_{g}", align_bytes=64)
-            scale_bytes = sb.tile([P, V_GROUP], U8, name=f"c_bytes_{g}", align_bytes=64)
-            quantize(nc, words[:], scale_bytes[:], woven[:])
-            staged = sb.tile([P, N // P, V_GROUP], F32, name=f"staged_{g}")
-            for mt in range(N // P):
-                second_pass(1, words[:], scale_bytes[:], g, mt)
-                if g == groups - 1 and mt == 1:
-                    nc.vector.tensor_copy(staged[:, mt, :], res[g, mt][:])
-                else:
-                    nc.scalar.copy(staged[:, mt, :], res[g, mt][:])
-            nc.sync.dma_start(
-                out[:, g * V_GROUP : (g + 1) * V_GROUP].rearrange("(a p) v -> p a v", p=P), staged[:]
-            )
+        def store(v0, width, shared):
+            staged = sb.tile([P, N // P, width], F32, name=f"staged_{v0}")
+            for c0 in range(0, width, V_GROUP):
+                for mt in range(N // P):
+                    src = res[(v0 + c0) // V_GROUP, mt][:]
+                    if shared and mt == 1:
+                        nc.vector.tensor_copy(staged[:, mt, c0 : c0 + V_GROUP], src)
+                    else:
+                        nc.scalar.copy(staged[:, mt, c0 : c0 + V_GROUP], src)
+            nc.sync.dma_start(out[:, v0 : v0 + width].rearrange("(a p) v -> p a v", p=P), staged[:])
 
-        cols = V_GROUP // LIST_ROWS
-        wovens = []
-        for g in range(groups):
-            last = g == groups - 1
-            if last:
-                quantize(nc, z_words[:], z_bytes[:], z_woven[:])
-                for zg in range(groups):
-                    vc = slice(zg * V_GROUP, (zg + 1) * V_GROUP)
-                    for mt in range(N // P):
-                        res[zg, mt] = psum.tile([P, V_GROUP], F32, name=f"res_{zg}_{mt}", tag=f"bank_{zg}_{mt}")
-                        second_pass(0, z_words[:, vc], z_bytes[:, vc], zg, mt)
-            planes = sb.tile([P, PACK, V_GROUP], BF16, name=f"centre_{g}", tag=plane_tags[g], align_bytes=64)
-            for t in range(PACK):
-                nc.vector.tensor_copy(planes[:, t, :], h[t][:].indirect(cen_sb[:, g * cols : (g + 1) * cols]))
-            woven = sb.tile([P, V_GROUP, PACK], BF16, name=f"c_woven_{g}", tag=woven_tags[g], align_bytes=64)
-            dst, src = weave_views(woven[:], planes[:])
-            if last:
-                nc.vector.tensor_copy(dst, src)
-            else:
-                nc.scalar.copy(dst, src)
-            wovens.append(woven)
-        for g in range(groups):
-            finish(g, wovens[g])
+        (v_a, n_a), (v_b, n_b), (v_c, n_c) = V_SLICES
+        planes_a = sb.tile([P, PACK, n_a], BF16, name="planes_a", align_bytes=64)
+        largest = sb.tile([P, PACK, V], BF16, name="largest", align_bytes=64)
+        last = PACK - 1
+        near = [sb.tile([P, last, V], BF16, name=f"near_{d}", align_bytes=64) for d in range(2)]
+        near_last = [sb.tile([P, V], BF16, name=f"near_last_{d}", tag=f"near_last_{d}", align_bytes=64) for d in range(2)]
+        for t in range(last):
+            for d, pos_sb in enumerate((pos1_sb, pos2_sb)):
+                nc.vector.tensor_copy(near[d][:, t, :], h[t][:].indirect(pos_sb[:]))
+            gather_centres(planes_a, t, v_a, n_a)
+        nc.vector.tensor_tensor(largest[:, 0:last, :], near[0][:], near[1][:], MAX)
+        gather_centres(planes_a, last, v_a, n_a)
+        for d, pos_sb in enumerate((pos1_sb, pos2_sb)):
+            nc.vector.tensor_copy(near_last[d][:], h[last][:].indirect(pos_sb[:]))
+        codes_a = quantized("a", weave(nc.scalar.copy, "woven_a", planes_a, n_a), n_a)
+        nc.vector.tensor_tensor(largest[:, last, :], near_last[0][:], near_last[1][:], MAX)
+        woven_z = weave(nc.scalar.copy, "woven_z", largest, V)
+
+        planes_b = sb.tile([P, PACK, n_b], BF16, name="planes_b", tag="near_last_0", align_bytes=64)
+        for t in range(PACK):
+            gather_centres(planes_b, t, v_b, n_b)
+        woven_b = weave(nc.scalar.copy, "woven_b", planes_b, n_b)
+
+        second_pass(0, quantized("z", woven_z, V), V, 0)
+        second_pass(1, codes_a, n_a, v_a)
+        store(v_a, n_a, False)
+
+        planes_c = sb.tile([P, PACK, n_c], BF16, name="planes_c", tag="woven_z", align_bytes=64)
+        for t in range(PACK):
+            gather_centres(planes_c, t, v_c, n_c)
+        second_pass(1, quantized("b", woven_b, n_b), n_b, v_b)
+        woven_c = weave(nc.vector.tensor_copy, "woven_c", planes_c, n_c)
+        store(v_b, n_b, False)
+        second_pass(1, quantized("c", woven_c, n_c), n_c, v_c)
+        store(v_c, n_c, True)

@@ -21,19 +21,28 @@ P = 128
 PACK = 4
 K_PASS = P * PACK
 PASSES = K // K_PASS
+QUADRANT = 32
+SCALE_ROWS = 4
 BANK = 512
+HALVES = S // BANK
 LIST_ROWS = 16
-X_CHUNKS = ((1024, 512, 512), (512, 512, 512, 256, 128, 128))
-W_CHUNKS = ((128, 128, 256), (256, 256))
-MIN_SHARE = 128
-V_GROUP = 128
-V_SLICES = ((0, 128), (128, 256), (384, 128))
+RUN = 4
+M_TILES = N // P
+GROUP = 128
+WARM_UP_PASSES = 3
+
+X_LOADS = (
+    ((512, 384), (512, 384), (512, 384), (512, 256)),
+    ((512, 384), (512, 256), (512, 256), (256, 128), (128, 128), (128, 0)),
+)
+W_LOADS = ((128, 128, 256), (256, 256))
+SLICE_A, SLICE_B, SLICE_C = (0, 128), (128, 256), (384, 128)
 
 
 def weave_views(woven, planes):
     return (
-        woven.rearrange("p (c i) j -> p c j i", i=4),
-        planes.rearrange("p j (c i) -> p c j i", i=4),
+        woven.rearrange("p (c r) j -> p c j r", r=RUN),
+        planes.rearrange("p j (c r) -> p c j r", r=RUN),
     )
 
 
@@ -49,229 +58,228 @@ def tile_picked_sagecat_max_e_kernel(
         sb = ctx.enter_context(tc.tile_pool(name="sb", bufs=1))
         psum = ctx.enter_context(tc.psum_pool(name="psum", bufs=1))
 
-        def list_tile(name, src):
-            t = sb.tile(list(src.shape), U16, name=name)
-            nc.sync.dma_start(t[:], src)
-            return t
+        def load_list(name, src):
+            tile = sb.tile(list(src.shape), U16, name=name)
+            nc.sync.dma_start(tile[:], src)
+            return tile
 
-        x_raw = []
-        offs_sb = None
-        for z in range(PASSES):
-            rows = xT[z * K_PASS : (z + 1) * K_PASS, :].rearrange("(p j) c -> p j c", j=PACK)
-            c0 = 0
-            for width in X_CHUNKS[z]:
-                raw = sb.tile([P, PACK, width], F32, name=f"x_raw_{z}_{c0}")
+        def load_x(g):
+            rows = xT[g * K_PASS : (g + 1) * K_PASS, :].rearrange("(p j) c -> p j c", j=PACK)
+            loads, c0 = [], 0
+            for width, on_scalar in X_LOADS[g]:
+                raw = sb.tile([P, PACK, width], F32, name=f"x_raw_{g}_{c0}")
                 nc.sync.dma_start(raw[:], rows[:, :, c0 : c0 + width])
-                x_raw.append((z, c0, width, raw))
+                loads.append((c0, width, on_scalar, raw))
                 c0 = c0 + width
-            if z == 0:
-                offs_sb = list_tile("offs_sb", offs)
-        w_raw = []
-        for z in range(PASSES):
-            rows = w1[z * K_PASS : (z + 1) * K_PASS, :].rearrange("(p j) c -> p j c", j=PACK)
-            c0 = 0
-            for width in W_CHUNKS[z]:
-                raw = sb.tile([P, PACK, width], F32, name=f"w_raw_{z}_{c0}", tag=f"w_raw_{z}_{c0}", align_bytes=64)
+            return loads
+
+        def load_w1(g):
+            rows = w1[g * K_PASS : (g + 1) * K_PASS, :].rearrange("(p j) c -> p j c", j=PACK)
+            loads, c0 = [], 0
+            for width in W_LOADS[g]:
+                raw = sb.tile([P, PACK, width], F32, name=f"w_raw_{g}_{c0}", tag=f"w_raw_{g}_{c0}", align_bytes=64)
                 nc.sync.dma_start(raw[:], rows[:, :, c0 : c0 + width])
-                w_raw.append((z, c0, width, raw))
+                loads.append((c0, width, raw))
                 c0 = c0 + width
-        pos1_sb = list_tile("pos1_sb", pos1)
-        pos2_sb = list_tile("pos2_sb", pos2)
-        cen_sb = list_tile("cen_sb", cen)
+            return loads
+
+        x_loads = [load_x(0)]
+        offs_sb = load_list("offs_sb", offs)
+        x_loads.append(load_x(1))
+        w_loads = [load_w1(g) for g in range(PASSES)]
+        last_w_tag = [f"w_raw_{g}_{H - W_LOADS[g][-1]}" for g in range(PASSES)]
+        pos_sb = [load_list("pos1_sb", pos1), load_list("pos2_sb", pos2)]
+        cen_sb = load_list("cen_sb", cen)
 
         x_bytes = sb.tile([P, T], U8, name="x_bytes", align_bytes=64)
         nc.gpsimd.memset(x_bytes[:], 0)
-        fp4_words, fp4_bytes = [], []
-        for name, words, scales in (("w3", w3_words, w3_scales), ("w2", w2_words, w2_scales)):
-            wt = sb.tile([P, 2 * N], U8, name=name + "_words", align_bytes=64)
-            nc.sync.dma_start(wt[:].bitcast(I32), words[0].bitcast(I32))
-            st = sb.tile([P, N], U8, name=name + "_bytes", align_bytes=64)
-            nc.gpsimd.memset(st[:], 0)
-            for q in range(4):
+
+        def load_fp4(name, words, scales):
+            words_sb = sb.tile([P, 2 * N], U8, name=name + "_words", align_bytes=64)
+            nc.sync.dma_start(words_sb[:].bitcast(I32), words[0].bitcast(I32))
+            bytes_sb = sb.tile([P, N], U8, name=name + "_bytes", align_bytes=64)
+            nc.gpsimd.memset(bytes_sb[:], 0)
+            for q in range(P // QUADRANT):
                 nc.sync.dma_start(
-                    st[32 * q : 32 * q + 4, :].bitcast(I32), scales[0, 4 * q : 4 * q + 4, :].bitcast(I32)
+                    bytes_sb[QUADRANT * q : QUADRANT * q + SCALE_ROWS, :].bitcast(I32),
+                    scales[0, SCALE_ROWS * q : SCALE_ROWS * (q + 1), :].bitcast(I32),
                 )
-            fp4_words.append(wt)
-            fp4_bytes.append(st)
+            return words_sb, bytes_sb
 
-        x_words = [sb.tile([P, T], U32, name=f"x_words_{z}", align_bytes=64) for z in range(PASSES)]
-        g_words = [sb.tile([P, S], U32, name="g_words_0", align_bytes=64)]
-        g_bytes = sb.tile([P, S], U8, name="g_bytes", align_bytes=64)
-        for z, c0, width, raw in x_raw:
-            if width > MIN_SHARE:
-                shares = ((width // 2, width // 2, True), (0, width // 2, False))
-            else:
-                shares = ((0, width, c0 + width == T),)
-            rounded = []
-            for lo, n, on_vector in shares:
-                woven = sb.tile([P, n, PACK], BF16, name=f"x_woven_{z}_{c0 + lo}", align_bytes=64)
-                dst, src = weave_views(woven[:], raw[:, :, lo : lo + n])
-                if on_vector:
-                    nc.vector.tensor_copy(dst, src)
-                else:
-                    nc.scalar.activation(dst, src, COPY)
-                rounded.append((c0 + lo, n, woven))
-            for lo, n, woven in rounded:
-                quantize(nc, x_words[z][:, lo : lo + n], x_bytes[4 * z : P, lo : lo + n], woven[:])
-            if z == 0 and c0 + width == T:
-                nc.vector.tensor_copy(g_words[0][:], x_words[0][:].indirect(offs_sb[:]))
+        w3_sb = load_fp4("w3", w3_words, w3_scales)
+        w2_sb = load_fp4("w2", w2_words, w2_scales)
 
-        w_woven = [sb.tile([P, PACK, P, PACK], BF16, name=f"w_woven_{z}", tag=f"w_woven_{z}", align_bytes=64) for z in range(PASSES)]
+        x_words = [sb.tile([P, T], U32, name=f"x_words_{g}", align_bytes=64) for g in range(PASSES)]
+        picked_words_0 = sb.tile([P, S], U32, name="picked_words_0", align_bytes=64)
+        picked_bytes = sb.tile([P, S], U8, name="picked_bytes", align_bytes=64)
 
-        w_words = [sb.tile([P, H], U32, name=f"w_words_{z}", align_bytes=64) for z in range(PASSES)]
+        def quantize_x(g):
+            for c0, width, on_scalar, raw in x_loads[g]:
+                woven = sb.tile([P, width, PACK], BF16, name=f"x_woven_{g}_{c0}", align_bytes=64)
+                if on_scalar > 0:
+                    nc.scalar.activation(*weave_views(woven[:, 0:on_scalar, :], raw[:, :, 0:on_scalar]), COPY)
+                if on_scalar < width:
+                    nc.vector.tensor_copy(*weave_views(woven[:, on_scalar:width, :], raw[:, :, on_scalar:width]))
+                nodes = slice(c0, c0 + width)
+                quantize(nc, x_words[g][:, nodes], x_bytes[SCALE_ROWS * g : P, nodes], woven[:])
+
+        quantize_x(0)
+        nc.vector.tensor_copy(picked_words_0[:], x_words[0][:].indirect(offs_sb[:]))
+        quantize_x(1)
+
+        w_woven = [sb.tile([P, PACK, P, PACK], BF16, name=f"w_woven_{g}", align_bytes=64) for g in range(PASSES)]
+        w_words = [sb.tile([P, H], U32, name=f"w_words_{g}", align_bytes=64) for g in range(PASSES)]
         w_bytes = {}
 
-        def quantize_w1(z, t0, t1, scale_bytes):
-            wc = slice(t0 * P, t1 * P)
-            quantize(nc, w_words[z][:, wc], scale_bytes[:, wc], w_woven[z][:, t0:t1].rearrange("p t m j -> p (t m) j"))
+        def quantize_w1(g, t0, t1, bytes_sb):
+            cols = slice(t0 * P, t1 * P)
+            quantize(nc, w_words[g][:, cols], bytes_sb[:, cols], w_woven[g][:, t0:t1].rearrange("p t m j -> p (t m) j"))
             for t in range(t0, t1):
-                w_bytes[z, t] = scale_bytes[:, t * P : (t + 1) * P]
+                w_bytes[g, t] = bytes_sb[:, t * P : (t + 1) * P]
 
-        for z, c0, width, raw in w_raw:
-            m0, m1 = c0 // PACK, (c0 + width) // PACK
-            nc.scalar.activation(
-                w_woven[z][:, :, m0:m1, :].rearrange("p t m j -> p m j t"),
-                raw[:].rearrange("p j (m t) -> p m j t", t=PACK),
-                COPY,
-            )
+        for g in range(PASSES):
+            for c0, width, raw in w_loads[g]:
+                nc.scalar.activation(
+                    w_woven[g][:, :, c0 // PACK : (c0 + width) // PACK, :].rearrange("p t m j -> p m j t"),
+                    raw[:].rearrange("p j (m t) -> p m j t", t=PACK),
+                    COPY,
+                )
 
-        nc.vector.tensor_copy(g_bytes[:], x_bytes[:].indirect(offs_sb[:]))
-        cols = BANK // LIST_ROWS
-        late_words = []
-        for half, tag in enumerate(("late_words_0", f"w_raw_0_{H - W_CHUNKS[0][-1]}")):
-            if half == 1:
-                quantize_w1(0, 0, 1, sb.tile([P, P], U8, name="w_bytes_first", align_bytes=64))
-            picked = sb.tile([P, BANK], U32, name=f"late_words_{half}", tag=tag, align_bytes=64)
-            nc.vector.tensor_copy(picked[:], x_words[1][:].indirect(offs_sb[:, half * cols : (half + 1) * cols]))
-            late_words.append(picked)
-        w_bytes_late = sb.tile([P, H], U8, name="w_bytes_late", align_bytes=64)
-        w_bytes_rest = sb.tile([P, H], U8, name="w_bytes_rest", tag=f"w_raw_1_{H - W_CHUNKS[1][-1]}", align_bytes=64)
-        quantize_w1(1, 0, 1, w_bytes_late)
+        nc.vector.tensor_copy(picked_bytes[:], x_bytes[:].indirect(offs_sb[:]))
+
+        def gather_words_1(half, tag):
+            picked = sb.tile([P, BANK], U32, name=f"picked_words_1_{half}", tag=tag, align_bytes=64)
+            entries = offs_sb[:, half * BANK // LIST_ROWS : (half + 1) * BANK // LIST_ROWS]
+            nc.vector.tensor_copy(picked[:], x_words[1][:].indirect(entries))
+            return picked
+
+        picked_words_1 = [gather_words_1(0, "picked_words_1_0")]
+        quantize_w1(0, 0, 1, sb.tile([P, P], U8, name="w_bytes_0_first", align_bytes=64))
+        picked_words_1.append(gather_words_1(1, last_w_tag[0]))
+        w_bytes_1 = sb.tile([P, H], U8, name="w_bytes_1", align_bytes=64)
+        w_bytes_0_rest = sb.tile([P, H], U8, name="w_bytes_0_rest", tag=last_w_tag[1], align_bytes=64)
+        quantize_w1(1, 0, 1, w_bytes_1)
         for t0, t1 in ((1, 2), (2, PACK)):
-            quantize_w1(1, t0, t1, w_bytes_late)
-            quantize_w1(0, t0, t1, w_bytes_rest)
+            quantize_w1(1, t0, t1, w_bytes_1)
+            quantize_w1(0, t0, t1, w_bytes_0_rest)
 
-        warm = psum.tile([P, BANK], F32, name="warm", tag="bank_3_1")
-        for rep in range(3):
+        warm_up = psum.tile([P, BANK], F32, name="warm_up", tag=f"bank_{PACK - 1}_{HALVES - 1}")
+        for turn in range(WARM_UP_PASSES):
             nc.tensor.matmul_mx(
-                out=warm[:],
-                lhsT=g_words[0][:, 0:P].bitcast(FP8X4),
-                lhsT_scale=g_bytes[:, 0:P],
-                rhs=g_words[0][:, 0:BANK].bitcast(FP8X4),
-                rhs_scale=g_bytes[:, 0:BANK],
+                out=warm_up[:],
+                lhsT=picked_words_0[:, 0:P].bitcast(FP8X4),
+                lhsT_scale=picked_bytes[:, 0:P],
+                rhs=picked_words_0[:, 0:BANK].bitcast(FP8X4),
+                rhs_scale=picked_bytes[:, 0:BANK],
                 start=True,
                 stop=True,
             )
         acc = [
-            [psum.tile([P, BANK], F32, name=f"acc_{t}_{half}", tag=f"bank_{t}_{half}") for half in range(2)]
+            [psum.tile([P, BANK], F32, name=f"acc_{t}_{half}", tag=f"bank_{t}_{half}") for half in range(HALVES)]
             for t in range(PACK)
         ]
         h = [sb.tile([P, S], F32, name=f"h_{t}") for t in range(PACK)]
 
-        def first_pass(z, t, half, opens):
-            wc = slice(t * P, (t + 1) * P)
-            xc = slice(half * BANK, (half + 1) * BANK)
+        def hidden_pass(g, t, half, opens):
+            nodes = slice(half * BANK, (half + 1) * BANK)
             nc.tensor.matmul_mx(
                 out=acc[t][half][:],
-                lhsT=w_words[z][:, wc].bitcast(FP8X4),
-                lhsT_scale=w_bytes[z, t],
-                rhs=(g_words[0][:, xc] if z == 0 else late_words[half][:]).bitcast(FP8X4),
-                rhs_scale=g_bytes[4 * z : P, xc],
+                lhsT=w_words[g][:, t * P : (t + 1) * P].bitcast(FP8X4),
+                lhsT_scale=w_bytes[g, t],
+                rhs=(picked_words_0[:, nodes] if g == 0 else picked_words_1[half][:]).bitcast(FP8X4),
+                rhs_scale=picked_bytes[SCALE_ROWS * g : P, nodes],
                 start=opens,
                 stop=not opens,
             )
 
-        for half in range(2):
-            first_pass(0, 0, half, True)
+        for half in range(HALVES):
+            hidden_pass(0, 0, half, True)
         for t in range(PACK):
-            for half in range(2):
+            for half in range(HALVES):
                 if t == 0:
-                    first_pass(1, t, half, False)
+                    hidden_pass(1, t, half, False)
                 else:
-                    first_pass(1, t, half, True)
-                    first_pass(0, t, half, False)
-                dst = h[t][:, half * BANK : (half + 1) * BANK]
-                nc.scalar.activation(dst, acc[t][half][:], RELU)
+                    hidden_pass(1, t, half, True)
+                    hidden_pass(0, t, half, False)
+                nc.scalar.activation(h[t][:, half * BANK : (half + 1) * BANK], acc[t][half][:], RELU)
 
-        def gather_centres(planes, t, v0, width):
-            nc.vector.tensor_copy(
-                planes[:, t, :], h[t][:].indirect(cen_sb[:, v0 // LIST_ROWS : (v0 + width) // LIST_ROWS])
-            )
+        def centre_planes(name, tag, targets):
+            return sb.tile([P, PACK, targets[1]], BF16, name=name, tag=tag, align_bytes=64)
 
-        def weave(engine_copy, name, planes, width):
-            woven = sb.tile([P, width, PACK], BF16, name=name, tag=name, align_bytes=64)
-            dst, src = weave_views(woven[:], planes[:])
-            engine_copy(dst, src)
+        def gather_centres(planes, t, targets):
+            v0, width = targets
+            entries = cen_sb[:, v0 // LIST_ROWS : (v0 + width) // LIST_ROWS]
+            nc.vector.tensor_copy(planes[:, t, :], h[t][:].indirect(entries))
+
+        def weave(copy_on_engine, name, planes):
+            woven = sb.tile([P, planes.shape[2], PACK], BF16, name=name, align_bytes=64)
+            copy_on_engine(*weave_views(woven[:], planes[:]))
             return woven
 
-        def quantized(name, woven, width):
-            words = sb.tile([P, width], U32, name=name + "_words", align_bytes=64)
-            scale_bytes = sb.tile([P, width], U8, name=name + "_bytes", align_bytes=64)
+        def quantized(name, woven):
+            words = sb.tile([P, woven.shape[1]], U32, name=name + "_words", align_bytes=64)
+            scale_bytes = sb.tile([P, woven.shape[1]], U8, name=name + "_bytes", align_bytes=64)
             quantize(nc, words[:], scale_bytes[:], woven[:])
             return words, scale_bytes
 
         res = {}
 
-        def second_pass(which, codes, width, v0):
-            words, scale_bytes = codes
-            for c0 in range(0, width, V_GROUP):
-                g = (v0 + c0) // V_GROUP
-                for mt in range(N // P):
-                    if which == 0:
-                        res[g, mt] = psum.tile([P, V_GROUP], F32, name=f"res_{g}_{mt}", tag=f"bank_{g}_{mt}")
+        def output_pass(weights, codes, targets, opens):
+            (w_words_sb, w_bytes_sb), (words, scale_bytes), (v0, width) = weights, codes, targets
+            for c0 in range(0, width, GROUP):
+                group = (v0 + c0) // GROUP
+                for mt in range(M_TILES):
+                    if opens:
+                        res[group, mt] = psum.tile([P, GROUP], F32, name=f"res_{group}_{mt}", tag=f"bank_{group}_{mt}")
                     nc.tensor.matmul_mx(
-                        out=res[g, mt][:],
-                        lhsT=fp4_words[which][:, 2 * P * mt : 2 * P * (mt + 1)].bitcast(FP4X4),
-                        lhsT_scale=fp4_bytes[which][:, P * mt : P * (mt + 1)],
-                        rhs=words[:, c0 : c0 + V_GROUP].bitcast(FP8X4),
-                        rhs_scale=scale_bytes[:, c0 : c0 + V_GROUP],
-                        start=(which == 0),
-                        stop=(which == 1),
+                        out=res[group, mt][:],
+                        lhsT=w_words_sb[:, 2 * P * mt : 2 * P * (mt + 1)].bitcast(FP4X4),
+                        lhsT_scale=w_bytes_sb[:, P * mt : P * (mt + 1)],
+                        rhs=words[:, c0 : c0 + GROUP].bitcast(FP8X4),
+                        rhs_scale=scale_bytes[:, c0 : c0 + GROUP],
+                        start=opens,
+                        stop=not opens,
                     )
 
-        def store(v0, width, shared):
-            staged = sb.tile([P, N // P, width], F32, name=f"staged_{v0}")
-            for c0 in range(0, width, V_GROUP):
-                for mt in range(N // P):
-                    src = res[(v0 + c0) // V_GROUP, mt][:]
-                    if shared and mt == 1:
-                        nc.vector.tensor_copy(staged[:, mt, c0 : c0 + V_GROUP], src)
-                    else:
-                        nc.scalar.copy(staged[:, mt, c0 : c0 + V_GROUP], src)
-            nc.sync.dma_start(out[:, v0 : v0 + width].rearrange("(a p) v -> p a v", p=P), staged[:])
+        def store(targets, copies):
+            v0, width = targets
+            staged = sb.tile([P, M_TILES, width], F32, name=f"staged_{v0}")
+            for c0 in range(0, width, GROUP):
+                for mt in range(M_TILES):
+                    copies[mt](staged[:, mt, c0 : c0 + GROUP], res[(v0 + c0) // GROUP, mt][:])
+            nc.sync.dma_start(out[:, v0 : v0 + width].rearrange("(mt p) v -> p mt v", p=P), staged[:])
 
-        (v_a, n_a), (v_b, n_b), (v_c, n_c) = V_SLICES
-        planes_a = sb.tile([P, PACK, n_a], BF16, name="planes_a", align_bytes=64)
-        largest = sb.tile([P, PACK, V], BF16, name="largest", align_bytes=64)
+        planes_a = centre_planes("planes_a", "planes_a", SLICE_A)
+        largest = sb.tile([P, PACK, V], BF16, name="largest", tag="largest", align_bytes=64)
         last = PACK - 1
         near = [sb.tile([P, last, V], BF16, name=f"near_{d}", align_bytes=64) for d in range(2)]
-        near_last = [sb.tile([P, V], BF16, name=f"near_last_{d}", tag=f"near_last_{d}", align_bytes=64) for d in range(2)]
+        near_last = [sb.tile([P, V], BF16, name=f"near_last_{d}", align_bytes=64) for d in range(2)]
         for t in range(last):
-            for d, pos_sb in enumerate((pos1_sb, pos2_sb)):
-                nc.vector.tensor_copy(near[d][:, t, :], h[t][:].indirect(pos_sb[:]))
-            gather_centres(planes_a, t, v_a, n_a)
+            for d in range(2):
+                nc.vector.tensor_copy(near[d][:, t, :], h[t][:].indirect(pos_sb[d][:]))
+            gather_centres(planes_a, t, SLICE_A)
         nc.vector.tensor_tensor(largest[:, 0:last, :], near[0][:], near[1][:], MAX)
-        gather_centres(planes_a, last, v_a, n_a)
-        for d, pos_sb in enumerate((pos1_sb, pos2_sb)):
-            nc.vector.tensor_copy(near_last[d][:], h[last][:].indirect(pos_sb[:]))
-        codes_a = quantized("a", weave(nc.scalar.copy, "woven_a", planes_a, n_a), n_a)
+        gather_centres(planes_a, last, SLICE_A)
+        for d in range(2):
+            nc.vector.tensor_copy(near_last[d][:], h[last][:].indirect(pos_sb[d][:]))
+        codes_a = quantized("a", weave(nc.scalar.copy, "woven_a", planes_a))
         nc.vector.tensor_tensor(largest[:, last, :], near_last[0][:], near_last[1][:], MAX)
-        woven_z = weave(nc.scalar.copy, "woven_z", largest, V)
+        woven_z = weave(nc.scalar.copy, "woven_z", largest)
 
-        planes_b = sb.tile([P, PACK, n_b], BF16, name="planes_b", tag="near_last_0", align_bytes=64)
+        planes_b = centre_planes("planes_b", "planes_a", SLICE_B)
         for t in range(PACK):
-            gather_centres(planes_b, t, v_b, n_b)
-        woven_b = weave(nc.scalar.copy, "woven_b", planes_b, n_b)
+            gather_centres(planes_b, t, SLICE_B)
+        woven_b = weave(nc.scalar.copy, "woven_b", planes_b)
 
-        second_pass(0, quantized("z", woven_z, V), V, 0)
-        second_pass(1, codes_a, n_a, v_a)
-        store(v_a, n_a, False)
+        output_pass(w3_sb, quantized("z", woven_z), (0, V), True)
+        output_pass(w2_sb, codes_a, SLICE_A, False)
+        store(SLICE_A, (nc.scalar.copy, nc.scalar.copy))
 
-        planes_c = sb.tile([P, PACK, n_c], BF16, name="planes_c", tag="woven_z", align_bytes=64)
+        planes_c = centre_planes("planes_c", "largest", SLICE_C)
         for t in range(PACK):
-            gather_centres(planes_c, t, v_c, n_c)
-        second_pass(1, quantized("b", woven_b, n_b), n_b, v_b)
-        woven_c = weave(nc.vector.tensor_copy, "woven_c", planes_c, n_c)
-        store(v_b, n_b, False)
-        second_pass(1, quantized("c", woven_c, n_c), n_c, v_c)
-        store(v_c, n_c, True)
+            gather_centres(planes_c, t, SLICE_C)
+        output_pass(w2_sb, quantized("b", woven_b), SLICE_B, False)
+        woven_c = weave(nc.vector.tensor_copy, "woven_c", planes_c)
+        store(SLICE_B, (nc.scalar.copy, nc.scalar.copy))
+        output_pass(w2_sb, quantized("c", woven_c), SLICE_C, False)
+        store(SLICE_C, (nc.scalar.copy, nc.vector.tensor_copy))

@@ -29,13 +29,10 @@ LIST_ROWS = 16
 RUN = 4
 M_TILES = N // P
 GROUP = 128
-WARM_UP_PASSES = 3
 
-X_LOADS = (
-    ((512, 384), (512, 384), (512, 384), (512, 256)),
-    ((512, 384), (512, 256), (512, 256), (256, 128), (128, 128), (128, 0)),
-)
-W_LOADS = ((128, 128, 256), (256, 256))
+X_LOADS = ((1024, 512, 512), (1024, 512, 256, 256))
+W_LOAD = 256
+QUANTIZE_NODES = 512
 SLICE_A, SLICE_B, SLICE_C = (0, 128), (128, 256), (384, 128)
 
 
@@ -66,28 +63,27 @@ def tile_picked_sagecat_max_e_kernel(
         def load_x(g):
             rows = xT[g * K_PASS : (g + 1) * K_PASS, :].rearrange("(p j) c -> p j c", j=PACK)
             loads, c0 = [], 0
-            for width, on_scalar in X_LOADS[g]:
+            for width in X_LOADS[g]:
                 raw = sb.tile([P, PACK, width], F32, name=f"x_raw_{g}_{c0}")
                 nc.sync.dma_start(raw[:], rows[:, :, c0 : c0 + width])
-                loads.append((c0, width, on_scalar, raw))
+                loads.append((c0, width, raw))
                 c0 = c0 + width
             return loads
 
         def load_w1(g):
             rows = w1[g * K_PASS : (g + 1) * K_PASS, :].rearrange("(p j) c -> p j c", j=PACK)
-            loads, c0 = [], 0
-            for width in W_LOADS[g]:
-                raw = sb.tile([P, PACK, width], F32, name=f"w_raw_{g}_{c0}", tag=f"w_raw_{g}_{c0}", align_bytes=64)
-                nc.sync.dma_start(raw[:], rows[:, :, c0 : c0 + width])
-                loads.append((c0, width, raw))
-                c0 = c0 + width
+            loads = []
+            for c0 in range(0, H, W_LOAD):
+                raw = sb.tile([P, PACK, W_LOAD], F32, name=f"w_raw_{g}_{c0}", tag=f"w_raw_{g}_{c0}", align_bytes=64)
+                nc.sync.dma_start(raw[:], rows[:, :, c0 : c0 + W_LOAD])
+                loads.append((c0, raw))
             return loads
 
         x_loads = [load_x(0)]
         offs_sb = load_list("offs_sb", offs)
         x_loads.append(load_x(1))
         w_loads = [load_w1(g) for g in range(PASSES)]
-        last_w_tag = [f"w_raw_{g}_{H - W_LOADS[g][-1]}" for g in range(PASSES)]
+        last_w_tag = [f"w_raw_{g}_{H - W_LOAD}" for g in range(PASSES)]
         pos_sb = [load_list("pos1_sb", pos1), load_list("pos2_sb", pos2)]
         cen_sb = load_list("cen_sb", cen)
 
@@ -114,14 +110,15 @@ def tile_picked_sagecat_max_e_kernel(
         picked_bytes = sb.tile([P, S], U8, name="picked_bytes", align_bytes=64)
 
         def quantize_x(g):
-            for c0, width, on_scalar, raw in x_loads[g]:
+            for c0, width, raw in x_loads[g]:
+                share = width // 2
                 woven = sb.tile([P, width, PACK], BF16, name=f"x_woven_{g}_{c0}", align_bytes=64)
-                if on_scalar > 0:
-                    nc.scalar.activation(*weave_views(woven[:, 0:on_scalar, :], raw[:, :, 0:on_scalar]), COPY)
-                if on_scalar < width:
-                    nc.vector.tensor_copy(*weave_views(woven[:, on_scalar:width, :], raw[:, :, on_scalar:width]))
-                nodes = slice(c0, c0 + width)
-                quantize(nc, x_words[g][:, nodes], x_bytes[SCALE_ROWS * g : P, nodes], woven[:])
+                nc.scalar.activation(*weave_views(woven[:, 0:share, :], raw[:, :, 0:share]), COPY)
+                nc.vector.tensor_copy(*weave_views(woven[:, share:width, :], raw[:, :, share:width]))
+                step = min(width, QUANTIZE_NODES)
+                for lo in reversed(range(0, width, step)):
+                    nodes = slice(c0 + lo, c0 + lo + step)
+                    quantize(nc, x_words[g][:, nodes], x_bytes[SCALE_ROWS * g : P, nodes], woven[:, lo : lo + step, :])
 
         quantize_x(0)
         nc.vector.tensor_copy(picked_words_0[:], x_words[0][:].indirect(offs_sb[:]))
@@ -138,9 +135,9 @@ def tile_picked_sagecat_max_e_kernel(
                 w_bytes[g, t] = bytes_sb[:, t * P : (t + 1) * P]
 
         for g in range(PASSES):
-            for c0, width, raw in w_loads[g]:
+            for c0, raw in w_loads[g]:
                 nc.scalar.activation(
-                    w_woven[g][:, :, c0 // PACK : (c0 + width) // PACK, :].rearrange("p t m j -> p m j t"),
+                    w_woven[g][:, :, c0 // PACK : (c0 + W_LOAD) // PACK, :].rearrange("p t m j -> p m j t"),
                     raw[:].rearrange("p j (m t) -> p m j t", t=PACK),
                     COPY,
                 )
@@ -163,17 +160,6 @@ def tile_picked_sagecat_max_e_kernel(
             quantize_w1(1, t0, t1, w_bytes_1)
             quantize_w1(0, t0, t1, w_bytes_0_rest)
 
-        warm_up = psum.tile([P, BANK], F32, name="warm_up", tag=f"bank_{PACK - 1}_{HALVES - 1}")
-        for turn in range(WARM_UP_PASSES):
-            nc.tensor.matmul_mx(
-                out=warm_up[:],
-                lhsT=picked_words_0[:, 0:P].bitcast(FP8X4),
-                lhsT_scale=picked_bytes[:, 0:P],
-                rhs=picked_words_0[:, 0:BANK].bitcast(FP8X4),
-                rhs_scale=picked_bytes[:, 0:BANK],
-                start=True,
-                stop=True,
-            )
         acc = [
             [psum.tile([P, BANK], F32, name=f"acc_{t}_{half}", tag=f"bank_{t}_{half}") for half in range(HALVES)]
             for t in range(PACK)

from contextlib import ExitStack

import concourse.mybir as mybir

K, T, S, V, H, N = 1024, 2048, 1024, 512, 512, 256
FLOPS = 2 * K * H * S + 2 * 2 * H * N * V

F32 = mybir.dt.float32
BF16 = mybir.dt.bfloat16
U32 = mybir.dt.uint32
I32 = mybir.dt.int32
U16 = mybir.dt.uint16
U8 = mybir.dt.uint8
FP8X4 = mybir.dt.float8_e4m3fn_x4
FP4X4 = mybir.dt.float4_e2m1fn_x4
COPY = mybir.ActivationFunctionType.Copy
RELU = mybir.ActivationFunctionType.Relu
MAX = mybir.AluOpType.max

P = 128
PACK = 4
K_PASS = P * PACK
PASSES = K // K_PASS
QUADRANT = 32
SCALE_ROWS = 4
BANK = 512
HALVES = S // BANK
LIST_ROWS = 16
RUN = 4
M_TILES = N // P
GROUP = 128

X_LOADS = ((1024, 512, 512), (1024, 512, 256, 256))
W_LOAD = 256
QUANTIZE_NODES = 512
SLICE_A, SLICE_B, SLICE_C = (0, 128), (128, 256), (384, 128)


def weave_views(woven, planes):
    return (
        woven.rearrange("p (c r) j -> p c j r", r=RUN),
        planes.rearrange("p j (c r) -> p c j r", r=RUN),
    )


def quantize(nc, words, scale_bytes, woven):
    nc.vector.quantize_mx(out=words.bitcast(FP8X4), scales=scale_bytes, in_=woven.rearrange("p c j -> p (c j)"))


def tile_picked_sagecat_max_e_kernel(
    tc, xT, w1, w2_words, w2_scales, w3_words, w3_scales, offs, cen, pos1, pos2, out
):
    nc = tc.nc
    with ExitStack() as ctx:
        sb = ctx.enter_context(tc.tile_pool(name="sb", bufs=1))
        psum = ctx.enter_context(tc.psum_pool(name="psum", bufs=1))

        def load_list(name, src):
            tile = sb.tile(list(src.shape), U16, name=name)
            nc.sync.dma_start(tile[:], src)
            return tile

        def load_x(g):
            rows = xT[g * K_PASS : (g + 1) * K_PASS, :].rearrange("(p j) c -> p j c", j=PACK)
            loads, c0 = [], 0
            for width in X_LOADS[g]:
                raw = sb.tile([P, PACK, width], F32, name=f"x_raw_{g}_{c0}")
                nc.sync.dma_start(raw[:], rows[:, :, c0 : c0 + width])
                loads.append((c0, width, raw))
                c0 = c0 + width
            return loads

        def load_w1(g):
            rows = w1[g * K_PASS : (g + 1) * K_PASS, :].rearrange("(p j) c -> p j c", j=PACK)
            loads = []
            for c0 in range(0, H, W_LOAD):
                raw = sb.tile([P, PACK, W_LOAD], F32, name=f"w_raw_{g}_{c0}", tag=f"w_raw_{g}_{c0}", align_bytes=64)
                nc.sync.dma_start(raw[:], rows[:, :, c0 : c0 + W_LOAD])
                loads.append((c0, raw))
            return loads

        x_loads = [load_x(0)]
        offs_sb = load_list("offs_sb", offs)
        x_loads.append(load_x(1))
        w_loads = [load_w1(g) for g in range(PASSES)]
        last_w_tag = [f"w_raw_{g}_{H - W_LOAD}" for g in range(PASSES)]
        pos_sb = [load_list("pos1_sb", pos1), load_list("pos2_sb", pos2)]
        cen_sb = load_list("cen_sb", cen)

        x_bytes = sb.tile([P, T], U8, name="x_bytes", align_bytes=64)
        nc.gpsimd.memset(x_bytes[:], 0)

        def load_fp4(name, words, scales):
            words_sb = sb.tile([P, 2 * N], U8, name=name + "_words", align_bytes=64)
            nc.sync.dma_start(words_sb[:].bitcast(I32), words[0].bitcast(I32))
            bytes_sb = sb.tile([P, N], U8, name=name + "_bytes", align_bytes=64)
            nc.gpsimd.memset(bytes_sb[:], 0)
            for q in range(P // QUADRANT):
                nc.sync.dma_start(
                    bytes_sb[QUADRANT * q : QUADRANT * q + SCALE_ROWS, :].bitcast(I32),
                    scales[0, SCALE_ROWS * q : SCALE_ROWS * (q + 1), :].bitcast(I32),
                )
            return words_sb, bytes_sb

        w3_sb = load_fp4("w3", w3_words, w3_scales)
        w2_sb = load_fp4("w2", w2_words, w2_scales)

        x_words = [sb.tile([P, T], U32, name=f"x_words_{g}", align_bytes=64) for g in range(PASSES)]
        picked_words_0 = sb.tile([P, S], U32, name="picked_words_0", align_bytes=64)
        picked_bytes = sb.tile([P, S], U8, name="picked_bytes", align_bytes=64)

        def quantize_x(g):
            for c0, width, raw in x_loads[g]:
                share = width // 2
                woven = sb.tile([P, width, PACK], BF16, name=f"x_woven_{g}_{c0}", align_bytes=64)
                nc.scalar.activation(*weave_views(woven[:, 0:share, :], raw[:, :, 0:share]), COPY)
                nc.vector.tensor_copy(*weave_views(woven[:, share:width, :], raw[:, :, share:width]))
                step = min(width, QUANTIZE_NODES)
                for lo in reversed(range(0, width, step)):
                    nodes = slice(c0 + lo, c0 + lo + step)
                    quantize(nc, x_words[g][:, nodes], x_bytes[SCALE_ROWS * g : P, nodes], woven[:, lo : lo + step, :])

        quantize_x(0)
        nc.vector.tensor_copy(picked_words_0[:], x_words[0][:].indirect(offs_sb[:]))
        quantize_x(1)

        w_woven = [sb.tile([P, PACK, P, PACK], BF16, name=f"w_woven_{g}", align_bytes=64) for g in range(PASSES)]
        w_words = [sb.tile([P, H], U32, name=f"w_words_{g}", align_bytes=64) for g in range(PASSES)]
        w_bytes = {}

        def quantize_w1(g, t0, t1, bytes_sb):
            cols = slice(t0 * P, t1 * P)
            quantize(nc, w_words[g][:, cols], bytes_sb[:, cols], w_woven[g][:, t0:t1].rearrange("p t m j -> p (t m) j"))
            for t in range(t0, t1):
                w_bytes[g, t] = bytes_sb[:, t * P : (t + 1) * P]

        for g in range(PASSES):
            for c0, raw in w_loads[g]:
                nc.scalar.activation(
                    w_woven[g][:, :, c0 // PACK : (c0 + W_LOAD) // PACK, :].rearrange("p t m j -> p m j t"),
                    raw[:].rearrange("p j (m t) -> p m j t", t=PACK),
                    COPY,
                )

        nc.vector.tensor_copy(picked_bytes[:], x_bytes[:].indirect(offs_sb[:]))

        def gather_words_1(half, tag):
            picked = sb.tile([P, BANK], U32, name=f"picked_words_1_{half}", tag=tag, align_bytes=64)
            entries = offs_sb[:, half * BANK // LIST_ROWS : (half + 1) * BANK // LIST_ROWS]
            nc.vector.tensor_copy(picked[:], x_words[1][:].indirect(entries))
            return picked

        picked_words_1 = [gather_words_1(0, "picked_words_1_0")]
        quantize_w1(0, 0, 1, sb.tile([P, P], U8, name="w_bytes_0_first", align_bytes=64))
        picked_words_1.append(gather_words_1(1, last_w_tag[0]))
        w_bytes_1 = sb.tile([P, H], U8, name="w_bytes_1", align_bytes=64)
        w_bytes_0_rest = sb.tile([P, H], U8, name="w_bytes_0_rest", tag=last_w_tag[1], align_bytes=64)
        quantize_w1(1, 0, 1, w_bytes_1)
        for t0, t1 in ((1, 2), (2, PACK)):
            quantize_w1(1, t0, t1, w_bytes_1)
            quantize_w1(0, t0, t1, w_bytes_0_rest)

        acc = [
            [psum.tile([P, BANK], F32, name=f"acc_{t}_{half}", tag=f"bank_{t}_{half}") for half in range(HALVES)]
            for t in range(PACK)
        ]
        h = [sb.tile([P, S], F32, name=f"h_{t}") for t in range(PACK)]

        def hidden_pass(g, t, half, opens):
            nodes = slice(half * BANK, (half + 1) * BANK)
            nc.tensor.matmul_mx(
                out=acc[t][half][:],
                lhsT=w_words[g][:, t * P : (t + 1) * P].bitcast(FP8X4),
                lhsT_scale=w_bytes[g, t],
                rhs=(picked_words_0[:, nodes] if g == 0 else picked_words_1[half][:]).bitcast(FP8X4),
                rhs_scale=picked_bytes[SCALE_ROWS * g : P, nodes],
                start=opens,
                stop=not opens,
            )

        for half in range(HALVES):
            hidden_pass(0, 0, half, True)
        for t in range(PACK):
            for half in range(HALVES):
                if t == 0:
                    hidden_pass(1, t, half, False)
                else:
                    hidden_pass(1, t, half, True)
                    hidden_pass(0, t, half, False)
                nc.scalar.activation(h[t][:, half * BANK : (half + 1) * BANK], acc[t][half][:], RELU)

        def centre_planes(name, tag, targets):
            return sb.tile([P, PACK, targets[1]], BF16, name=name, tag=tag, align_bytes=64)

        def gather_centres(planes, t, targets):
            v0, width = targets
            entries = cen_sb[:, v0 // LIST_ROWS : (v0 + width) // LIST_ROWS]
            nc.vector.tensor_copy(planes[:, t, :], h[t][:].indirect(entries))

        def weave(copy_on_engine, name, planes):
            woven = sb.tile([P, planes.shape[2], PACK], BF16, name=name, align_bytes=64)
            copy_on_engine(*weave_views(woven[:], planes[:]))
            return woven

        def quantized(name, woven):
            words = sb.tile([P, woven.shape[1]], U32, name=name + "_words", align_bytes=64)
            scale_bytes = sb.tile([P, woven.shape[1]], U8, name=name + "_bytes", align_bytes=64)
            quantize(nc, words[:], scale_bytes[:], woven[:])
            return words, scale_bytes

        res = {}

        def output_pass(weights, codes, targets, opens):
            (w_words_sb, w_bytes_sb), (words, scale_bytes), (v0, width) = weights, codes, targets
            for c0 in range(0, width, GROUP):
                group = (v0 + c0) // GROUP
                for mt in range(M_TILES):
                    if opens:
                        res[group, mt] = psum.tile([P, GROUP], F32, name=f"res_{group}_{mt}", tag=f"bank_{group}_{mt}")
                    nc.tensor.matmul_mx(
                        out=res[group, mt][:],
                        lhsT=w_words_sb[:, 2 * P * mt : 2 * P * (mt + 1)].bitcast(FP4X4),
                        lhsT_scale=w_bytes_sb[:, P * mt : P * (mt + 1)],
                        rhs=words[:, c0 : c0 + GROUP].bitcast(FP8X4),
                        rhs_scale=scale_bytes[:, c0 : c0 + GROUP],
                        start=opens,
                        stop=not opens,
                    )

        def store(targets, copies):
            v0, width = targets
            staged = sb.tile([P, M_TILES, width], F32, name=f"staged_{v0}")
            for c0 in range(0, width, GROUP):
                for mt in range(M_TILES):
                    copies[mt](staged[:, mt, c0 : c0 + GROUP], res[(v0 + c0) // GROUP, mt][:])
            nc.sync.dma_start(out[:, v0 : v0 + width].rearrange("(mt p) v -> p mt v", p=P), staged[:])

        planes_a = centre_planes("planes_a", "planes_a", SLICE_A)
        largest = sb.tile([P, PACK, V], BF16, name="largest", tag="largest", align_bytes=64)
        last = PACK - 1
        near = [sb.tile([P, last, V], BF16, name=f"near_{d}", align_bytes=64) for d in range(2)]
        near_last = [sb.tile([P, V], BF16, name=f"near_last_{d}", align_bytes=64) for d in range(2)]
        for t in range(last):
            for d in range(2):
                nc.vector.tensor_copy(near[d][:, t, :], h[t][:].indirect(pos_sb[d][:]))
            gather_centres(planes_a, t, SLICE_A)
        nc.vector.tensor_tensor(largest[:, 0:last, :], near[0][:], near[1][:], MAX)
        gather_centres(planes_a, last, SLICE_A)
        for d in range(2):
            nc.vector.tensor_copy(near_last[d][:], h[last][:].indirect(pos_sb[d][:]))
        codes_a = quantized("a", weave(nc.scalar.copy, "woven_a", planes_a))
        nc.vector.tensor_tensor(largest[:, last, :], near_last[0][:], near_last[1][:], MAX)
        woven_z = weave(nc.scalar.copy, "woven_z", largest)

        planes_b = centre_planes("planes_b", "planes_a", SLICE_B)
        for t in range(PACK):
            gather_centres(planes_b, t, SLICE_B)
        woven_b = weave(nc.scalar.copy, "woven_b", planes_b)

        output_pass(w3_sb, quantized("z", woven_z), (0, V), True)
        output_pass(w2_sb, codes_a, SLICE_A, False)
        store(SLICE_A, (nc.scalar.copy, nc.scalar.copy))

        planes_c = centre_planes("planes_c", "largest", SLICE_C)
        for t in range(PACK):
            gather_centres(planes_c, t, SLICE_C)
        output_pass(w2_sb, quantized("b", woven_b), SLICE_B, False)
        woven_c = weave(nc.vector.tensor_copy, "woven_c", planes_c)
        store(SLICE_B, (nc.scalar.copy, nc.scalar.copy))
        output_pass(w2_sb, quantized("c", woven_c), SLICE_C, False)
        store(SLICE_C, (nc.scalar.copy, nc.vector.tensor_copy))
